import numpy as np
CORES = [20,21,28,29]
N = 4
def setup_inputs(rng):
    return {"x": rng.standard_normal((N, 128, 4), dtype=np.float32)}
def reference(x):
    s = np.maximum.accumulate(x, axis=0)
    y = np.full(x.shape, np.nan, x.dtype)
    y[1:] = s[:-1]
    return {"y": y}

from concourse.bass import DstId, RemoteDMATransfer

SCRATCH = {
    "own": ("dram", [128, 4], "float32"),
    "left": ("dram", [128, 4], "float32"),
    "more": ("dram", [128, 4], "float32"),
}
SEMAPHORES = ["loaded", "arrived", "sent", "stored"]

ENGINE = 0x1
MAX = 2


def rank_program(g, core, T, topo):
    r0, r1, r2, r3 = T.cores
    gate = topo.chip(r1) * topo.CORES_PER_CHIP + 6
    sem = T.sem

    def dst(c):
        rid, pid, _se = topo.addr(c)
        return DstId(rid=rid, pnc=pid)

    def send(srcs, targets, out, alu_op):
        g.remote_dma_fused(
            [RemoteDMATransfer(dst_ids=[dst(c) for c in targets], dma_engine_mask=ENGINE, remote_sem=sem.arrived,
                               srcs=srcs, dsts=[out[:] for _c in targets], alu_op=alu_op)],
            local_sem=sem.sent)

    def stage():
        g.sync.dma_start(T.own[:], T.x[:]).then_inc(sem.loaded, 16)
        g.wait_ge(sem.loaded, 16)

    def store():
        g.scalar.wait_ge(sem.arrived, 1)
        g.scalar.dma_start(T.y[:], T.left[:]).then_inc(sem.stored, 16)
        g.scalar.wait_ge(sem.stored, 16)

    if core == r0:
        stage()
        send([T.own[:]], [r1, gate], T.left, 0)
        g.wait_ge(sem.sent, 1)
    elif core == r1:
        store()
        stage()
        send([T.own[:]], [gate], T.more, 0)
        g.wait_ge(sem.sent, 1)
    elif core == gate:
        g.wait_ge(sem.arrived, 2)
        send([T.left[:], T.more[:]], [r2], T.left, MAX)
        g.wait_ge(sem.sent, 1)
    elif core == r2:
        store()
        stage()
        g.wait_ge(sem.arrived, 1)
        send([T.left[:], T.own[:]], [r3], T.left, MAX)
        g.wait_ge(sem.sent, 1)
    elif core == r3:
        store()
